import numpy as np
import ml_dtypes


def mxq(x, axis, fmt="e4m3"):
    dtype, down = {"e4m3": (ml_dtypes.float8_e4m3fn, 7), "e5m2": (ml_dtypes.float8_e5m2, 14)}[fmt]
    v = np.moveaxis(np.asarray(x, np.float32).astype(ml_dtypes.bfloat16).astype(np.float64), axis, -1)
    blocks = v.reshape(v.shape[:-1] + (-1, 32))
    amax = np.abs(blocks).max(-1, keepdims=True)
    byte = np.maximum(np.where(amax > 0, np.frexp(amax)[1] - 1 + 127, 0) - down, 1)
    scale = np.exp2(byte - 127.0)
    codes = (blocks / scale).astype(np.float32).astype(dtype).astype(np.float64)
    return np.moveaxis((codes * scale).reshape(v.shape), -1, axis)


WIDE = False


def mx_kscale(k):
    if not WIDE:
        return np.ones(k)
    levels = np.array([10, -10, 5, -5, 0])
    if k % 512:
        return np.exp2(np.random.permutation(np.resize(levels, k // 32))).repeat(32)
    a = np.empty((k // 512, 16))
    for p in range(k // 512):
        a[p, :8] = np.random.permutation(np.resize(levels, 8))
        for g in range(8):
            far = levels[np.abs(levels - a[p, g]) >= 10]
            a[p, g + 8] = far[np.random.randint(len(far))]
    return np.exp2(a.ravel()).repeat(32)


def f64(x):
    return np.asarray(x).astype(np.float64)


def striped(idx):
    return np.tile(idx.reshape(-1, 16).T, (8, 1)).astype(np.uint16)


def unstriped(offs):
    return offs[:16].T.reshape(-1).astype(np.int64)


E2M1 = np.array([0.0, 0.5, 1.0, 1.5, 2.0, 3.0, 4.0, 6.0, -0.0, -0.5, -1.0, -1.5, -2.0, -3.0, -4.0, -6.0])


def pack_weight(w, fmt):
    k, n = w.shape
    w = f64(np.asarray(w, np.float32).astype(ml_dtypes.bfloat16)).reshape(k // 32, 32, n)
    amax = np.abs(w).max(1)
    if fmt == "e4m3":
        byte = np.frexp(amax)[1] - 1 + 127 - 7
    else:
        mant, ex = np.frexp(amax / 6.0)
        byte = np.where(mant > 0.5, ex, ex - 1) + 127
    byte = np.clip(np.where(amax > 0, byte, 1), 1, 254)
    scaled = (w * np.exp2(127.0 - byte)[:, None, :]).reshape(k, n).astype(np.float32)
    by_word = np.ascontiguousarray(scaled.reshape(k // 512, 128, 4, n).transpose(0, 1, 3, 2))
    if fmt == "e4m3":
        words = by_word.astype(ml_dtypes.float8_e4m3fn).view(np.uint8)
    else:
        c = by_word.astype(ml_dtypes.float4_e2m1fn).view(np.uint8) & 0xF
        words = (c[..., 0::2] | (c[..., 1::2] << 4)).reshape(k // 512, 128, 2 * n)
    return np.ascontiguousarray(words), np.ascontiguousarray(byte.astype(np.uint8).reshape(k // 512, 16, n))


def unpack_weight(words, scales, fmt):
    g, _, n = scales.shape
    words = np.ascontiguousarray(words).reshape(g, 128, n, -1)
    if fmt == "e4m3":
        vals = words.view(ml_dtypes.float8_e4m3fn).astype(np.float64)
    else:
        nib = np.empty((g, 128, n, 4), np.uint8)
        nib[..., 0::2] = words & 0xF
        nib[..., 1::2] = words >> 4
        vals = E2M1[nib]
    vals = vals * np.repeat(np.exp2(scales.astype(np.float64) - 127.0), 8, axis=1)[..., None]
    return vals.transpose(0, 1, 3, 2).reshape(g * 512, n)


def gelu(v):
    return 0.5 * v * (1.0 + np.tanh(np.sqrt(2.0 / np.pi) * (v + 0.044715 * v**3)))


def bf(x):
    return np.asarray(x, np.float32).astype(ml_dtypes.bfloat16)


def planes(Y):
    n, m = Y.shape
    b = f64(bf(Y)).reshape(n // 32, 32, m)
    amax = np.abs(b).max(1)
    byte = np.clip(np.where(amax > 0, np.frexp(amax)[1] - 1 + 127 - 7, 1), 1, 254)
    codes = (b * np.exp2(127.0 - byte)[:, None, :]).reshape(n, m).astype(np.float32).astype(ml_dtypes.float8_e4m3fn).view(np.uint8)
    words = codes.reshape(n // 512, 128, 4, m).transpose(0, 1, 3, 2)
    return np.ascontiguousarray(words), np.ascontiguousarray(byte.astype(np.uint8).reshape(n // 512, 16, m))


K, H, R, N, T, S = 512, 1024, 512, 512, 2048, 1024

def setup_inputs():
    n = np.random.standard_normal
    s = mx_kscale(K)[:, None]
    u = mx_kscale(H)[:, None]
    e = mx_kscale(R)[:, None]
    tab_words, tab_scales = pack_weight(n((K, T)) * s, "e4m3")
    w2_words, w2_scales = pack_weight(n((K, H)) / np.sqrt(K) / s * u.T, "e2m1")
    w4_words, w4_scales = pack_weight(n((H, N)) / np.sqrt(H) / u, "e4m3")
    w5_words, w5_scales = pack_weight(n((R, N)) / np.sqrt(R) / e, "e2m1")
    return {
        "tab_words": tab_words, "tab_scales": tab_scales,
        "offs": striped(np.random.permutation(T)[:S]),
        "w1": (n((K, H)) / np.sqrt(K) / s * u.T).astype(np.float32),
        "w2_words": w2_words, "w2_scales": w2_scales,
        "w3": (n((K, R)) / np.sqrt(K) / s).astype(np.float32),
        "w4_words": w4_words, "w4_scales": w4_scales,
        "w5_words": w5_words, "w5_scales": w5_scales,
        "ch1": n((H, S)).astype(np.float32),
        "ch2": n((H, S)).astype(np.float32),
        "gain": (np.exp(0.3 * n(R)) * e[:, 0]).astype(np.float32),
    }

def reference(tab_words, tab_scales, offs, w1, w2_words, w2_scales, w3, w4_words, w4_scales,
              w5_words, w5_scales, ch1, ch2, gain):
    v = unpack_weight(tab_words, tab_scales, "e4m3")[:, unstriped(offs)]
    w2 = unpack_weight(w2_words, w2_scales, "e2m1")
    w4 = unpack_weight(w4_words, w4_scales, "e4m3")
    w5 = unpack_weight(w5_words, w5_scales, "e2m1")
    a = mxq(f64(w1), 0, "e4m3").T @ v
    b = w2.T @ v
    h = a * f64(ch1) + b * f64(ch2)
    words, scales = planes(h)
    d = f64(gain)[:, None] * np.tanh(mxq(f64(w3), 0, "e4m3").T @ v)
    y = w4.T @ mxq(h, 0, "e4m3") + w5.T @ mxq(d, 0, "e4m3")
    return y, h, words, scales

@@ -1,0 +1,271 @@
+from contextlib import ExitStack
+
+import concourse.mybir as mybir
+
+K, H, R, N, T, S = 512, 1024, 512, 512, 2048, 1024
+FLOPS = 2 * S * (2 * K * H + K * R + H * N + R * N)
+
+F32 = mybir.dt.float32
+BF16 = mybir.dt.bfloat16
+I32 = mybir.dt.int32
+U32 = mybir.dt.uint32
+U16 = mybir.dt.uint16
+U8 = mybir.dt.uint8
+FP8X4 = mybir.dt.float8_e4m3fn_x4
+FP4X4 = mybir.dt.float4_e2m1fn_x4
+MULT = mybir.AluOpType.mult
+ADD = mybir.AluOpType.add
+TANH = mybir.ActivationFunctionType.Tanh
+
+P = 128
+PACK = 4
+PASS = P * PACK
+BANK = 512
+HALF = 512
+NARROW = 128
+
+
+def tile_list_relay_forward_log_kernel(tc, tab_words, tab_scales, offs, w1, w2_words, w2_scales, w3,
+                                                w4_words, w4_scales, w5_words, w5_scales, ch1, ch2, gain,
+                                                out_0, out_1, out_2, out_3):
+    nc = tc.nc
+    with ExitStack() as ctx:
+        keep = ctx.enter_context(tc.tile_pool(name="keep", bufs=1))
+        stage = ctx.enter_context(tc.tile_pool(name="stage", bufs=4))
+        ps_ab = ctx.enter_context(tc.psum_pool(name="ps_ab", bufs=4))
+        ps_c = ctx.enter_context(tc.psum_pool(name="ps_c", bufs=2))
+        ps_y = ctx.enter_context(tc.psum_pool(name="ps_y", bufs=2))
+
+        def held(name, shape, dtype):
+            return keep.tile(shape, dtype, name=name, align_bytes=64)
+
+        offsets = keep.tile([P, S // 16], U16, name="offsets")
+        tab_w = held("tab_w", [P, T], I32)
+        tab_s = held("tab_s", [P, T], U8)
+        w2_raw = held("w2_raw", [P, 2 * H], U8)
+        w2_raw_s = held("w2_raw_s", [P, H], U8)
+        w4_w = held("w4_w", [P, 2 * N], I32)
+        w4_s = held("w4_s", [P, 2 * N], U8)
+        w5_w = held("w5_w", [P, 2 * N], U8)
+        w5_s = held("w5_s", [P, N], U8)
+        gain_t = held("gain_t", [P, PACK], F32)
+
+        def load_scales(queue, plane, rows):
+            passes = rows.shape[0]
+            for q in range(4):
+                queue.dma_start(
+                    out=plane[32 * q:32 * q + 4, :].bitcast(I32).rearrange("p (a c) -> p a c", a=passes),
+                    in_=rows[:, 4 * q:4 * q + 4, :].bitcast(I32).rearrange("a q c -> q a c"))
+
+        def load_rows(name, src, rows, cols):
+            tile = held(name, [P, PACK, HALF], F32)
+            nc.sync.dma_start(out=tile[:], in_=src[rows, cols].rearrange("(p t) c -> p t c", t=PACK))
+            return tile
+
+        def span(i):
+            return slice(i * HALF, (i + 1) * HALF)
+
+        nc.gpsimd.memset(w2_raw_s[:].bitcast(I32), 0)
+        nc.vector.memset(tab_s[:].bitcast(I32), 0)
+        nc.gpsimd.memset(w5_s[:].bitcast(I32), 0)
+        nc.gpsimd.memset(w4_s[:].bitcast(I32), 0)
+        c1, c2, w1_raw = {}, {}, {}
+        nc.sync.dma_start(offsets[:], offs)
+        nc.sync.dma_start(out=w2_raw[:].bitcast(I32), in_=w2_words[0].bitcast(I32))
+        nc.sync.dma_start(out=gain_t[:], in_=gain.rearrange("(p t) -> p t", t=PACK))
+        load_scales(nc.sync, w2_raw_s, w2_scales)
+        nc.sync.dma_start(out=tab_w[:], in_=tab_words[0].rearrange("p t i -> p (t i)").bitcast(I32))
+        w1_raw[0] = load_rows("w1_0", w1, span(0), span(0))
+        load_scales(nc.sync, tab_s, tab_scales)
+
+        warm = held("warm", [P, 2], F32)
+        nc.vector.memset(warm[:, 0:1], 0.0)
+        nc.scalar.activation(out=warm[:, 1:2], in_=warm[:, 0:1], func=TANH)
+
+        c2[0, 0] = load_rows("ch2_00", ch2, span(0), span(0))
+        c1[0, 0] = load_rows("ch1_00", ch1, span(0), span(0))
+        w3_raw = load_rows("w3_raw", w3, span(0), span(0))
+        w1_raw[1] = load_rows("w1_1", w1, span(0), span(1))
+        nc.sync.dma_start(out=w5_w[:].bitcast(I32), in_=w5_words[0].bitcast(I32))
+        load_scales(nc.sync, w5_s, w5_scales)
+        c2[1, 0] = load_rows("ch2_10", ch2, span(1), span(0))
+        c1[1, 0] = load_rows("ch1_10", ch1, span(1), span(0))
+        nc.sync.dma_start(out=w4_w[:].rearrange("p (a c) -> p a c", a=2),
+                          in_=w4_words.rearrange("a p c i -> p a (c i)").bitcast(I32))
+        load_scales(nc.sync, w4_s, w4_scales)
+        c2[0, 1] = load_rows("ch2_01", ch2, span(0), span(1))
+        c1[0, 1] = load_rows("ch1_01", ch1, span(0), span(1))
+        c2[1, 1] = load_rows("ch2_11", ch2, span(1), span(1))
+        c1[1, 1] = load_rows("ch1_11", ch1, span(1), span(1))
+
+        w2_w = held("w2_w", [P, 2 * H], U8)
+        w2_s = held("w2_s", [P, H], U8)
+
+        def deal(dealt, raw, size):
+            nc.vector.tensor_copy(out=dealt[:].rearrange("p (g t m b) -> p g m t b", g=2, t=PACK, b=size),
+                                  in_=raw[:].rearrange("p (g m t b) -> p g m t b", g=2, t=PACK, b=size))
+
+        def gather(name, window, dtype, jh):
+            picked = held("%s%d" % (name, jh), [P, HALF], dtype)
+            nc.vector.tensor_copy(picked[:], window.indirect(offsets[:, jh * HALF // 16:(jh + 1) * HALF // 16]))
+            return picked
+
+        def quantize(words, scales, grouped):
+            nc.vector.quantize_mx(out=words.bitcast(FP8X4), scales=scales, in_=grouped)
+
+        def staged(width):
+            tile = stage.tile([P, PACK * HALF], BF16, name="staged", align_bytes=64)
+            return tile[:, 0:PACK * width]
+
+        def quantize_weight(name, raw):
+            grouped = staged(HALF)
+            nc.scalar.copy(out=grouped.rearrange("p (t m i) -> p m i t", t=PACK, i=PACK),
+                           in_=raw[:].rearrange("p i (m t) -> p m i t", t=PACK))
+            words = held(name + "_w", [P, PASS], U32)
+            scales = held(name + "_s", [P, PASS], U8)
+            quantize(words[:], scales[:], grouped)
+            return words, scales
+
+        def interleave(rows, width):
+            grouped = staged(width)
+            nc.scalar.copy(out=grouped.rearrange("p (c i t) -> p c t i", i=4, t=PACK),
+                           in_=rows.rearrange("p t (c i) -> p c t i", i=4))
+            return grouped
+
+        def fp8(words, scales, cols):
+            return words[:, cols].bitcast(FP8X4), scales[:, cols]
+
+        def fp4(words, scales, cols):
+            return words[:, 2 * cols.start:2 * cols.stop].bitcast(FP4X4), scales[:, cols]
+
+        def mm(out, lhs, rhs, start=True, stop=True):
+            nc.tensor.matmul_mx(out=out, lhsT=lhs[0], lhsT_scale=lhs[1], rhs=rhs[0], rhs_scale=rhs[1],
+                                start=start, stop=stop)
+
+        def times_channel(out, weight, chan, v, cols):
+            width = cols.stop - cols.start
+            per_bank = BANK // width
+            for t0 in range(0, PACK, per_bank):
+                bank = ps_ab.tile([P, BANK], F32, name="bank_ab")
+                for t in range(per_bank):
+                    mm(bank[:, t * width:(t + 1) * width], weight(t0 + t), fp8(v[0], v[1], cols))
+                nc.vector.tensor_tensor(out=out[:, t0:t0 + per_bank, :],
+                                        in0=bank[:].rearrange("p (t w) -> p t w", t=per_bank),
+                                        in1=chan[:, t0:t0 + per_bank, cols], op=MULT)
+
+        h_w = [held("h_w%d" % g, [P, S], U32) for g in range(2)]
+        h_s = held("h_s", [P, 2 * S], U8)
+        d_w = held("d_w", [P, S], U32)
+        d_s = held("d_s", [P, S], U8)
+        v, w1_q = {}, {}
+
+        def b_part(g, j0, width):
+            jh, cols = j0 // HALF, slice(j0 % HALF, j0 % HALF + width)
+            times_channel(c2[g, jh][:, :, cols],
+                          lambda t: fp4(w2_w, w2_s, slice(PASS * g + P * t, PASS * g + P * (t + 1))),
+                          c2[g, jh], v[jh], cols)
+
+        def a_part(g, j0, width):
+            jh, cols = j0 // HALF, slice(j0 % HALF, j0 % HALF + width)
+            h = held("h_%d_%d" % (g, j0), [P, PACK, width], F32)
+            times_channel(h, lambda t: fp8(w1_q[g][0], w1_q[g][1], slice(P * t, P * (t + 1))),
+                          c1[g, jh], v[jh], cols)
+            return h
+
+        def add_parts(g, j0, width, h):
+            jh, cols = j0 // HALF, slice(j0 % HALF, j0 % HALF + width)
+            for t0 in (0, 2):
+                nc.vector.tensor_tensor(out=h[:, t0:t0 + 2, :], in0=h[:, t0:t0 + 2, :],
+                                        in1=c2[g, jh][:, t0:t0 + 2, cols], op=ADD)
+            nc.sync.dma_start(out=out_1[span(g), j0:j0 + width].rearrange("(p t) j -> p t j", t=PACK), in_=h[:])
+            return interleave(h[:], width)
+
+        def h_planes(g, j0, width, grouped):
+            quantize(h_w[g][:, j0:j0 + width], h_s[:, S * g + j0:S * g + j0 + width], grouped)
+
+        def store_words(g, jh):
+            nc.sync.dma_start(out=out_2[g].rearrange("p m i -> p (m i)").bitcast(I32)[:, span(jh)],
+                              in_=h_w[g][:, span(jh)].bitcast(I32))
+
+        def side_tanh(jh, w3_q):
+            th = keep.tile([P, PACK, HALF], F32, name="th")
+            for t in range(PACK):
+                bank = ps_c.tile([P, BANK], F32, name="bank_c")
+                mm(bank[:], fp8(w3_q[0], w3_q[1], slice(P * t, P * (t + 1))), fp8(v[jh][0], v[jh][1], span(0)))
+                nc.scalar.activation(out=th[:, t, :], in_=bank[:], func=TANH)
+            return th
+
+        def side_gain(th):
+            db = keep.tile([P, PACK, HALF], BF16, name="db")
+            for t in range(PACK):
+                nc.vector.tensor_scalar_mul(out=db[:, t, :], in0=th[:, t, :], scalar1=gain_t[:, t:t + 1])
+            return interleave(db[:], HALF)
+
+        def passes(out, n, cols):
+            ncols = slice(P * n, P * (n + 1))
+            mm(out, fp4(w5_w, w5_s, ncols), fp8(d_w, d_s, cols), True, False)
+            for g in range(2):
+                gcols = slice(N * g + P * n, N * g + P * (n + 1))
+                mm(out, fp8(w4_w, w4_s, gcols),
+                   (h_w[g][:, cols].bitcast(FP8X4), h_s[:, S * g + cols.start:S * g + cols.stop]), False, g == 1)
+
+        def forward(j0, width):
+            y = held("y_%d" % j0, [P, 4, width], F32)
+            if width == HALF:
+                for n in range(4):
+                    bank = ps_y.tile([P, BANK], F32, name="bank_y")
+                    passes(bank[:], n, slice(j0, j0 + width))
+                    nc.scalar.copy(out=y[:, n, :], in_=bank[:])
+            else:
+                for c0 in range(0, width, NARROW):
+                    bank = ps_y.tile([P, BANK], F32, name="bank_y")
+                    for n in range(4):
+                        passes(bank[:, n * NARROW:(n + 1) * NARROW], n, slice(j0 + c0, j0 + c0 + NARROW))
+                    nc.scalar.copy(out=y[:, :, c0:c0 + NARROW], in_=bank[:].rearrange("p (n w) -> p n w", n=4))
+            nc.sync.dma_start(out=out_0[:, j0:j0 + width].rearrange("(n p) j -> p n j", p=P), in_=y[:])
+
+        deal(w2_w, w2_raw, 2)
+        deal(w2_s, w2_raw_s, 1)
+        v_w = [gather("v_w", tab_w[:].bitcast(U32), U32, jh) for jh in range(2)]
+        for jh in range(2):
+            v[jh] = (v_w[jh], gather("v_s", tab_s[:], U8, jh))
+        w1_q[0] = quantize_weight("w1q0", w1_raw[0])
+        b_part(0, 0, HALF)
+        h00 = a_part(0, 0, HALF)
+        w3_q = quantize_weight("w3q", w3_raw)
+        th0 = side_tanh(0, w3_q)
+        w1_q[1] = quantize_weight("w1q1", w1_raw[1])
+        hb00 = add_parts(0, 0, HALF, h00)
+        d0 = side_gain(th0)
+        b_part(1, 0, HALF)
+        th1 = side_tanh(1, w3_q)
+        h_planes(0, 0, HALF, hb00)
+        store_words(0, 0)
+        h10 = a_part(1, 0, HALF)
+        quantize(d_w[:, span(0)], d_s[:, span(0)], d0)
+        hb10 = add_parts(1, 0, HALF, h10)
+        d1 = side_gain(th1)
+        b_part(0, HALF, HALF)
+        h_planes(1, 0, HALF, hb10)
+        store_words(1, 0)
+        h01 = a_part(0, HALF, HALF)
+        quantize(d_w[:, span(1)], d_s[:, span(1)], d1)
+        hb01 = add_parts(0, HALF, HALF, h01)
+        pieces = [(HALF, 256), (HALF + 256, NARROW), (HALF + 384, NARROW)]
+        pending = None
+        for j0, width in pieces:
+            b_part(1, j0, width)
+            if pending is None:
+                forward(0, HALF)
+                h_planes(0, HALF, HALF, hb01)
+                store_words(0, 1)
+            else:
+                h_planes(1, *pending)
+                forward(pending[0], pending[1])
+            pending = (j0, width, add_parts(1, j0, width, a_part(1, j0, width)))
+        h_planes(1, *pending)
+        forward(pending[0], pending[1])
+        store_words(1, 1)
+        for q in range(4):
+            nc.sync.dma_start(out=out_3[:, 4 * q:4 * q + 4, :].bitcast(I32).rearrange("g q m -> q g m"),
+                              in_=h_s[32 * q:32 * q + 4, :].bitcast(I32).rearrange("p (g m) -> p g m", g=2))

@@ -16,6 +16,7 @@ FP4X4 = mybir.dt.float4_e2m1fn_x4
 MULT = mybir.AluOpType.mult
 ADD = mybir.AluOpType.add
 TANH = mybir.ActivationFunctionType.Tanh
+COPY = mybir.ActivationFunctionType.Copy
 
 P = 128
 PACK = 4
@@ -23,6 +24,16 @@ PASS = P * PACK
 BANK = 512
 HALF = 512
 NARROW = 128
+POOL_ADD = 0
+POOL_GAIN = 2
+POOL_DEAL = 0
+Y_ON_V = 1
+AB = 4
+W3_AT = 0
+DBHOLD = 0
+ILV = 1
+ONEADD = 1
+HOLDQ = 1
 
 
 def tile_list_relay_forward_log_kernel(tc, tab_words, tab_scales, offs, w1, w2_words, w2_scales, w3,
@@ -31,13 +42,15 @@ def tile_list_relay_forward_log_kernel(tc, tab_words, tab_scales, offs, w1, w2_w
     nc = tc.nc
     with ExitStack() as ctx:
         keep = ctx.enter_context(tc.tile_pool(name="keep", bufs=1))
-        stage = ctx.enter_context(tc.tile_pool(name="stage", bufs=4))
-        ps_ab = ctx.enter_context(tc.psum_pool(name="ps_ab", bufs=4))
-        ps_c = ctx.enter_context(tc.psum_pool(name="ps_c", bufs=2))
-        ps_y = ctx.enter_context(tc.psum_pool(name="ps_y", bufs=2))
+        psum = ctx.enter_context(tc.psum_pool(name="psum", bufs=1))
+        turns = {"ab": [], "cy": []}
 
-        def held(name, shape, dtype):
-            return keep.tile(shape, dtype, name=name, align_bytes=64)
+        def next_bank(ring, size):
+            turns[ring].append(ring)
+            return psum.tile([P, BANK], F32, name="%s%d" % (ring, len(turns[ring]) % size))
+
+        def held(name, shape, dtype, place=None):
+            return keep.tile(shape, dtype, name=name, tag=place or name, align_bytes=64)
 
         offsets = keep.tile([P, S // 16], U16, name="offsets")
         tab_w = held("tab_w", [P, T], I32)
@@ -65,35 +78,43 @@ def tile_list_relay_forward_log_kernel(tc, tab_words, tab_scales, offs, w1, w2_w
         def span(i):
             return slice(i * HALF, (i + 1) * HALF)
 
-        nc.gpsimd.memset(w2_raw_s[:].bitcast(I32), 0)
         nc.vector.memset(tab_s[:].bitcast(I32), 0)
+        nc.vector.memset(w2_raw_s[:].bitcast(I32), 0)
+        warm = held("warm", [P, 2], F32)
+        nc.gpsimd.memset(warm[:, 0:1], 0.0)
         nc.gpsimd.memset(w5_s[:].bitcast(I32), 0)
         nc.gpsimd.memset(w4_s[:].bitcast(I32), 0)
+        nc.scalar.activation(out=warm[:, 1:2], in_=warm[:, 0:1], func=TANH)
         c1, c2, w1_raw = {}, {}, {}
         nc.sync.dma_start(offsets[:], offs)
         nc.sync.dma_start(out=w2_raw[:].bitcast(I32), in_=w2_words[0].bitcast(I32))
         nc.sync.dma_start(out=gain_t[:], in_=gain.rearrange("(p t) -> p t", t=PACK))
-        load_scales(nc.sync, w2_raw_s, w2_scales)
         nc.sync.dma_start(out=tab_w[:], in_=tab_words[0].rearrange("p t i -> p (t i)").bitcast(I32))
+        nc.sync.dma_start(out=w5_w[:].bitcast(I32), in_=w5_words[0].bitcast(I32))
         w1_raw[0] = load_rows("w1_0", w1, span(0), span(0))
         load_scales(nc.sync, tab_s, tab_scales)
-
-        warm = held("warm", [P, 2], F32)
-        nc.vector.memset(warm[:, 0:1], 0.0)
-        nc.scalar.activation(out=warm[:, 1:2], in_=warm[:, 0:1], func=TANH)
-
-        c2[0, 0] = load_rows("ch2_00", ch2, span(0), span(0))
+        if W3_AT == 0:
+            w3_raw = load_rows("w3_raw", w3, span(0), span(0))
         c1[0, 0] = load_rows("ch1_00", ch1, span(0), span(0))
-        w3_raw = load_rows("w3_raw", w3, span(0), span(0))
+        if W3_AT == 3:
+            w3_raw = load_rows("w3_raw", w3, span(0), span(0))
+        if W3_AT in (1, 2):
+            c2[0, 0] = load_rows("ch2_00", ch2, span(0), span(0))
+        load_scales(nc.sync, w2_raw_s, w2_scales)
+        if W3_AT in (0, 3):
+            c2[0, 0] = load_rows("ch2_00", ch2, span(0), span(0))
+        if W3_AT == 1:
+            w3_raw = load_rows("w3_raw", w3, span(0), span(0))
         w1_raw[1] = load_rows("w1_1", w1, span(0), span(1))
-        nc.sync.dma_start(out=w5_w[:].bitcast(I32), in_=w5_words[0].bitcast(I32))
-        load_scales(nc.sync, w5_s, w5_scales)
         c2[1, 0] = load_rows("ch2_10", ch2, span(1), span(0))
+        if W3_AT == 2:
+            w3_raw = load_rows("w3_raw", w3, span(0), span(0))
+        load_scales(nc.sync, w5_s, w5_scales)
         c1[1, 0] = load_rows("ch1_10", ch1, span(1), span(0))
+        c2[0, 1] = load_rows("ch2_01", ch2, span(0), span(1))
         nc.sync.dma_start(out=w4_w[:].rearrange("p (a c) -> p a c", a=2),
                           in_=w4_words.rearrange("a p c i -> p a (c i)").bitcast(I32))
         load_scales(nc.sync, w4_s, w4_scales)
-        c2[0, 1] = load_rows("ch2_01", ch2, span(0), span(1))
         c1[0, 1] = load_rows("ch1_01", ch1, span(0), span(1))
         c2[1, 1] = load_rows("ch2_11", ch2, span(1), span(1))
         c1[1, 1] = load_rows("ch1_11", ch1, span(1), span(1))
@@ -101,9 +122,9 @@ def tile_list_relay_forward_log_kernel(tc, tab_words, tab_scales, offs, w1, w2_w
         w2_w = held("w2_w", [P, 2 * H], U8)
         w2_s = held("w2_s", [P, H], U8)
 
-        def deal(dealt, raw, size):
-            nc.vector.tensor_copy(out=dealt[:].rearrange("p (g t m b) -> p g m t b", g=2, t=PACK, b=size),
-                                  in_=raw[:].rearrange("p (g m t b) -> p g m t b", g=2, t=PACK, b=size))
+        def deal(engine, dealt, raw, size):
+            engine.tensor_copy(out=dealt.rearrange("p (g t m b) -> p g t m b", m=P, t=PACK, b=size),
+                               in_=raw.rearrange("p (g m t b) -> p g t m b", m=P, t=PACK, b=size))
 
         def gather(name, window, dtype, jh):
             picked = held("%s%d" % (name, jh), [P, HALF], dtype)
@@ -113,23 +134,23 @@ def tile_list_relay_forward_log_kernel(tc, tab_words, tab_scales, offs, w1, w2_w
         def quantize(words, scales, grouped):
             nc.vector.quantize_mx(out=words.bitcast(FP8X4), scales=scales, in_=grouped)
 
-        def staged(width):
-            tile = stage.tile([P, PACK * HALF], BF16, name="staged", align_bytes=64)
-            return tile[:, 0:PACK * width]
+        def staged(place, width):
+            tile = held(place, [P, PACK * width], BF16)
+            return tile[:]
 
-        def quantize_weight(name, raw):
-            grouped = staged(HALF)
+        def quantize_weight(name, raw, place, words_place=None):
+            grouped = staged(place, HALF)
             nc.scalar.copy(out=grouped.rearrange("p (t m i) -> p m i t", t=PACK, i=PACK),
                            in_=raw[:].rearrange("p i (m t) -> p m i t", t=PACK))
-            words = held(name + "_w", [P, PASS], U32)
+            words = held(name + "_w", [P, PASS], U32, words_place)
             scales = held(name + "_s", [P, PASS], U8)
             quantize(words[:], scales[:], grouped)
             return words, scales
 
-        def interleave(rows, width):
-            grouped = staged(width)
-            nc.scalar.copy(out=grouped.rearrange("p (c i t) -> p c t i", i=4, t=PACK),
-                           in_=rows.rearrange("p t (c i) -> p c t i", i=4))
+        def interleave(rows, width, place, copy=nc.scalar.copy):
+            grouped = staged(place, width)
+            copy(out=grouped.rearrange("p (c i t) -> p c t i", i=4, t=PACK),
+                 in_=rows.rearrange("p t (c i) -> p c t i", i=4))
             return grouped
 
         def fp8(words, scales, cols):
@@ -146,7 +167,7 @@ def tile_list_relay_forward_log_kernel(tc, tab_words, tab_scales, offs, w1, w2_w
             width = cols.stop - cols.start
             per_bank = BANK // width
             for t0 in range(0, PACK, per_bank):
-                bank = ps_ab.tile([P, BANK], F32, name="bank_ab")
+                bank = next_bank("ab", AB)
                 for t in range(per_bank):
                     mm(bank[:, t * width:(t + 1) * width], weight(t0 + t), fp8(v[0], v[1], cols))
                 nc.vector.tensor_tensor(out=out[:, t0:t0 + per_bank, :],
@@ -155,7 +176,7 @@ def tile_list_relay_forward_log_kernel(tc, tab_words, tab_scales, offs, w1, w2_w
 
         h_w = [held("h_w%d" % g, [P, S], U32) for g in range(2)]
         h_s = held("h_s", [P, 2 * S], U8)
-        d_w = held("d_w", [P, S], U32)
+        d_w = {}
         d_s = held("d_s", [P, S], U8)
         v, w1_q = {}, {}
 
@@ -172,13 +193,20 @@ def tile_list_relay_forward_log_kernel(tc, tab_words, tab_scales, offs, w1, w2_w
                           c1[g, jh], v[jh], cols)
             return h
 
-        def add_parts(g, j0, width, h):
+        def add_parts(g, j0, width, h, place):
             jh, cols = j0 // HALF, slice(j0 % HALF, j0 % HALF + width)
-            for t0 in (0, 2):
-                nc.vector.tensor_tensor(out=h[:, t0:t0 + 2, :], in0=h[:, t0:t0 + 2, :],
-                                        in1=c2[g, jh][:, t0:t0 + 2, cols], op=ADD)
+            on_pool = POOL_ADD if width == HALF else 0
+            for t in range(on_pool):
+                nc.gpsimd.tensor_tensor(out=h[:, t, :], in0=h[:, t, :], in1=c2[g, jh][:, t, cols], op=ADD)
+            step = PACK if (ONEADD and width < HALF) else 2
+            for t0 in range(on_pool, PACK, step):
+                t1 = min(t0 + step, PACK)
+                nc.vector.tensor_tensor(out=h[:, t0:t1, :], in0=h[:, t0:t1, :],
+                                        in1=c2[g, jh][:, t0:t1, cols], op=ADD)
             nc.sync.dma_start(out=out_1[span(g), j0:j0 + width].rearrange("(p t) j -> p t j", t=PACK), in_=h[:])
-            return interleave(h[:], width)
+            if j0 >= S - ILV * NARROW:
+                return interleave(h[:], width, place, nc.vector.tensor_copy)
+            return interleave(h[:], width, place)
 
         def h_planes(g, j0, width, grouped):
             quantize(h_w[g][:, j0:j0 + width], h_s[:, S * g + j0:S * g + j0 + width], grouped)
@@ -187,84 +215,134 @@ def tile_list_relay_forward_log_kernel(tc, tab_words, tab_scales, offs, w1, w2_w
             nc.sync.dma_start(out=out_2[g].rearrange("p m i -> p (m i)").bitcast(I32)[:, span(jh)],
                               in_=h_w[g][:, span(jh)].bitcast(I32))
 
-        def side_tanh(jh, w3_q):
-            th = keep.tile([P, PACK, HALF], F32, name="th")
+        def side_tanh(jh, w3_q, place):
+            th = held("th%d" % jh, [P, PACK, HALF], F32, place)
             for t in range(PACK):
-                bank = ps_c.tile([P, BANK], F32, name="bank_c")
+                bank = next_bank("cy", 8 - AB)
                 mm(bank[:], fp8(w3_q[0], w3_q[1], slice(P * t, P * (t + 1))), fp8(v[jh][0], v[jh][1], span(0)))
                 nc.scalar.activation(out=th[:, t, :], in_=bank[:], func=TANH)
             return th
 
-        def side_gain(th):
-            db = keep.tile([P, PACK, HALF], BF16, name="db")
+        def side_gain(th, place):
+            db = held("db", [P, PACK, HALF], BF16, "ch2_00" if DBHOLD else None)
             for t in range(PACK):
-                nc.vector.tensor_scalar_mul(out=db[:, t, :], in0=th[:, t, :], scalar1=gain_t[:, t:t + 1])
-            return interleave(db[:], HALF)
+                if POOL_GAIN == 2:
+                    nc.scalar.activation(out=db[:, t, :], in_=th[:, t, :], func=COPY, scale=gain_t[:, t:t + 1])
+                elif POOL_GAIN:
+                    nc.gpsimd.tensor_scalar(out=db[:, t, :], in0=th[:, t, :], scalar1=gain_t[:, t:t + 1],
+                                            scalar2=0.0, op0=MULT, op1=ADD)
+                else:
+                    nc.vector.tensor_scalar_mul(out=db[:, t, :], in0=th[:, t, :], scalar1=gain_t[:, t:t + 1])
+            return interleave(db[:], HALF, place)
 
-        def passes(out, n, cols):
-            ncols = slice(P * n, P * (n + 1))
-            mm(out, fp4(w5_w, w5_s, ncols), fp8(d_w, d_s, cols), True, False)
-            for g in range(2):
-                gcols = slice(N * g + P * n, N * g + P * (n + 1))
-                mm(out, fp8(w4_w, w4_s, gcols),
-                   (h_w[g][:, cols].bitcast(FP8X4), h_s[:, S * g + cols.start:S * g + cols.stop]), False, g == 1)
+        def d_planes(jh, grouped, place):
+            d_w[jh] = held("d_w%d" % jh, [P, HALF], U32, place)
+            quantize(d_w[jh][:], d_s[:, span(jh)], grouped)
 
-        def forward(j0, width):
+        def w4_pass(out, g, n, cols, stop):
+            mm(out, fp8(w4_w, w4_s, slice(N * g + P * n, N * g + P * (n + 1))),
+               (h_w[g][:, cols].bitcast(FP8X4), h_s[:, S * g + cols.start:S * g + cols.stop]), False, stop)
+
+        def w5_pass(out, n, cols, start):
+            mm(out, fp4(w5_w, w5_s, slice(P * n, P * (n + 1))),
+               (d_w[cols.start // HALF][:, cols.start % HALF:(cols.stop - 1) % HALF + 1].bitcast(FP8X4), d_s[:, cols]), start, False)
+
+        def store_y(y, cols):
+            nc.sync.dma_start(out=out_0[:, cols].rearrange("(n p) j -> p n j", p=P), in_=y[:])
+
+        def forward_wide(cols):
+            y = held("y_wide", [P, 4, HALF], F32)
+            for n in range(4):
+                bank = next_bank("cy", 8 - AB)
+                w5_pass(bank[:], n, cols, True)
+                for g in range(2):
+                    w4_pass(bank[:], g, n, cols, g == 1)
+                nc.scalar.copy(out=y[:, n, :], in_=bank[:])
+            store_y(y, cols)
+
+        def open_narrow(j0):
+            bank = next_bank("cy", 8 - AB)
+            cols = slice(j0, j0 + NARROW)
+            for n in range(4):
+                w5_pass(bank[:, n * NARROW:(n + 1) * NARROW], n, cols, n == 0)
+            for n in range(4):
+                w4_pass(bank[:, n * NARROW:(n + 1) * NARROW], 0, n, cols, False)
+            return bank
+
+        def close_narrow(j0, width, last):
             y = held("y_%d" % j0, [P, 4, width], F32)
-            if width == HALF:
+            for c0 in range(0, width, NARROW):
+                bank = narrow[j0 + c0]
                 for n in range(4):
-                    bank = ps_y.tile([P, BANK], F32, name="bank_y")
-                    passes(bank[:], n, slice(j0, j0 + width))
-                    nc.scalar.copy(out=y[:, n, :], in_=bank[:])
-            else:
-                for c0 in range(0, width, NARROW):
-                    bank = ps_y.tile([P, BANK], F32, name="bank_y")
-                    for n in range(4):
-                        passes(bank[:, n * NARROW:(n + 1) * NARROW], n, slice(j0 + c0, j0 + c0 + NARROW))
+                    w4_pass(bank[:, n * NARROW:(n + 1) * NARROW], 1, n, slice(j0 + c0, j0 + c0 + NARROW), n == 3)
+                if last and Y_ON_V:
+                    nc.vector.tensor_copy(out=y[:, :, c0:c0 + NARROW], in_=bank[:].rearrange("p (n w) -> p n w", n=4))
+                else:
                     nc.scalar.copy(out=y[:, :, c0:c0 + NARROW], in_=bank[:].rearrange("p (n w) -> p n w", n=4))
-            nc.sync.dma_start(out=out_0[:, j0:j0 + width].rearrange("(n p) j -> p n j", p=P), in_=y[:])
+            store_y(y, slice(j0, j0 + width))
 
-        deal(w2_w, w2_raw, 2)
-        deal(w2_s, w2_raw_s, 1)
+        deal(nc.vector, w2_w[:], w2_raw[:], 2)
         v_w = [gather("v_w", tab_w[:].bitcast(U32), U32, jh) for jh in range(2)]
         for jh in range(2):
             v[jh] = (v_w[jh], gather("v_s", tab_s[:], U8, jh))
-        w1_q[0] = quantize_weight("w1q0", w1_raw[0])
-        b_part(0, 0, HALF)
+        w1_q[0] = quantize_weight("w1q0", w1_raw[0], "stage_a", "tab_s" if HOLDQ else None)
+        if W3_AT == 0:
+            w3_q = quantize_weight("w3q", w3_raw, "stage_b")
         h00 = a_part(0, 0, HALF)
-        w3_q = quantize_weight("w3q", w3_raw)
-        th0 = side_tanh(0, w3_q)
-        w1_q[1] = quantize_weight("w1q1", w1_raw[1])
-        hb00 = add_parts(0, 0, HALF, h00)
-        d0 = side_gain(th0)
+        if POOL_DEAL:
+            for g in range(2):
+                deal(nc.gpsimd, w2_s[:, span(g)], w2_raw_s[:, span(g)], 1)
+        else:
+            deal(nc.vector, w2_s[:], w2_raw_s[:], 1)
+        if W3_AT == 3:
+            w3_q = quantize_weight("w3q", w3_raw, "stage_b")
+        if W3_AT in (0, 3):
+            th0 = side_tanh(0, w3_q, None)
+        b_part(0, 0, HALF)
+        if W3_AT == 1:
+            w3_q = quantize_weight("w3q", w3_raw, "stage_c", "ch1_00")
+        w1_q[1] = quantize_weight("w1q1", w1_raw[1], "stage_a")
+        hb00 = add_parts(0, 0, HALF, h00, "stage_b")
+        if W3_AT == 2:
+            w3_q = quantize_weight("w3q", w3_raw, "stage_c", "ch1_00")
         b_part(1, 0, HALF)
-        th1 = side_tanh(1, w3_q)
+        if W3_AT in (1, 2):
+            th0 = side_tanh(0, w3_q, None)
         h_planes(0, 0, HALF, hb00)
         store_words(0, 0)
+        d0 = side_gain(th0, "stage_b")
+        th1 = side_tanh(1, w3_q, "th0" if DBHOLD else "ch2_00")
         h10 = a_part(1, 0, HALF)
-        quantize(d_w[:, span(0)], d_s[:, span(0)], d0)
-        hb10 = add_parts(1, 0, HALF, h10)
-        d1 = side_gain(th1)
+        hb10 = add_parts(1, 0, HALF, h10, "stage_a")
+        d_planes(0, d0, "ch1_10")
         b_part(0, HALF, HALF)
         h_planes(1, 0, HALF, hb10)
         store_words(1, 0)
+        d1 = side_gain(th1, "stage_a")
         h01 = a_part(0, HALF, HALF)
-        quantize(d_w[:, span(1)], d_s[:, span(1)], d1)
-        hb01 = add_parts(0, HALF, HALF, h01)
+        forward_wide(span(0))
+        hb01 = add_parts(0, HALF, HALF, h01, "stage_b")
+        d_planes(1, d1, "ch1_01")
         pieces = [(HALF, 256), (HALF + 256, NARROW), (HALF + 384, NARROW)]
         pending = None
+        narrow = {}
         for j0, width in pieces:
             b_part(1, j0, width)
             if pending is None:
-                forward(0, HALF)
                 h_planes(0, HALF, HALF, hb01)
                 store_words(0, 1)
-            else:
+            h = a_part(1, j0, width)
+            if pending is not None:
                 h_planes(1, *pending)
-                forward(pending[0], pending[1])
-            pending = (j0, width, add_parts(1, j0, width, a_part(1, j0, width)))
+            grouped = add_parts(1, j0, width, h, "stage_%d" % j0)
+            if pending is None:
+                for c0 in range(HALF, S, NARROW):
+                    narrow[c0] = open_narrow(c0)
+            else:
+                close_narrow(pending[0], pending[1], False)
+            pending = (j0, width, grouped)
         h_planes(1, *pending)
-        forward(pending[0], pending[1])
+        close_narrow(pending[0], pending[1], True)
         store_words(1, 1)
         for q in range(4):
             nc.sync.dma_start(out=out_3[:, 4 * q:4 * q + 4, :].bitcast(I32).rearrange("g q m -> q g m"),

@@ -25,12 +25,20 @@ BANK = 512
 HALF = 512
 NARROW = 128
 POOL_ADD = 0
-POOL_GAIN = 2
+G0 = 2
+G1 = 2
+DB1 = None
+ILD1 = "stage_a"
+O3Q = 0
 POOL_DEAL = 0
 Y_ON_V = 1
 AB = 4
 W3_AT = 0
 DBHOLD = 0
+W2S = 1
+SPLITY = 0
+POOLQ = 0
+YFIRST = 0
 ILV = 1
 ONEADD = 1
 HOLDQ = 1
@@ -63,12 +71,15 @@ def tile_list_relay_forward_log_kernel(tc, tab_words, tab_scales, offs, w1, w2_w
         w5_s = held("w5_s", [P, N], U8)
         gain_t = held("gain_t", [P, PACK], F32)
 
+        def live_rows(plane, r, passes):
+            return plane[r:P:32, :].bitcast(I32).rearrange("p (a c) -> p a c", a=passes)
+
+        def scale_rows(rows, r):
+            return rows[:, r:16:4, :].bitcast(I32).rearrange("a q c -> q a c")
+
         def load_scales(queue, plane, rows):
-            passes = rows.shape[0]
-            for q in range(4):
-                queue.dma_start(
-                    out=plane[32 * q:32 * q + 4, :].bitcast(I32).rearrange("p (a c) -> p a c", a=passes),
-                    in_=rows[:, 4 * q:4 * q + 4, :].bitcast(I32).rearrange("a q c -> q a c"))
+            for r in range(4):
+                queue.dma_start(out=live_rows(plane, r, rows.shape[0]), in_=scale_rows(rows, r))
 
         def load_rows(name, src, rows, cols):
             tile = held(name, [P, PACK, HALF], F32)
@@ -95,12 +106,15 @@ def tile_list_relay_forward_log_kernel(tc, tab_words, tab_scales, offs, w1, w2_w
         load_scales(nc.sync, tab_s, tab_scales)
         if W3_AT == 0:
             w3_raw = load_rows("w3_raw", w3, span(0), span(0))
+        if W2S:
+            load_scales(nc.sync, w2_raw_s, w2_scales)
         c1[0, 0] = load_rows("ch1_00", ch1, span(0), span(0))
         if W3_AT == 3:
             w3_raw = load_rows("w3_raw", w3, span(0), span(0))
         if W3_AT in (1, 2):
             c2[0, 0] = load_rows("ch2_00", ch2, span(0), span(0))
-        load_scales(nc.sync, w2_raw_s, w2_scales)
+        if not W2S:
+            load_scales(nc.sync, w2_raw_s, w2_scales)
         if W3_AT in (0, 3):
             c2[0, 0] = load_rows("ch2_00", ch2, span(0), span(0))
         if W3_AT == 1:
@@ -109,12 +123,12 @@ def tile_list_relay_forward_log_kernel(tc, tab_words, tab_scales, offs, w1, w2_w
         c2[1, 0] = load_rows("ch2_10", ch2, span(1), span(0))
         if W3_AT == 2:
             w3_raw = load_rows("w3_raw", w3, span(0), span(0))
-        load_scales(nc.sync, w5_s, w5_scales)
+        load_scales(nc.gpsimd if POOLQ else nc.sync, w5_s, w5_scales)
         c1[1, 0] = load_rows("ch1_10", ch1, span(1), span(0))
         c2[0, 1] = load_rows("ch2_01", ch2, span(0), span(1))
         nc.sync.dma_start(out=w4_w[:].rearrange("p (a c) -> p a c", a=2),
                           in_=w4_words.rearrange("a p c i -> p a (c i)").bitcast(I32))
-        load_scales(nc.sync, w4_s, w4_scales)
+        load_scales(nc.gpsimd if POOLQ else nc.sync, w4_s, w4_scales)
         c1[0, 1] = load_rows("ch1_01", ch1, span(0), span(1))
         c2[1, 1] = load_rows("ch2_11", ch2, span(1), span(1))
         c1[1, 1] = load_rows("ch1_11", ch1, span(1), span(1))
@@ -135,7 +149,7 @@ def tile_list_relay_forward_log_kernel(tc, tab_words, tab_scales, offs, w1, w2_w
             nc.vector.quantize_mx(out=words.bitcast(FP8X4), scales=scales, in_=grouped)
 
         def staged(place, width):
-            tile = held(place, [P, PACK * width], BF16)
+            tile = held("staged", [P, PACK * width], BF16, place)
             return tile[:]
 
         def quantize_weight(name, raw, place, words_place=None):
@@ -223,8 +237,8 @@ def tile_list_relay_forward_log_kernel(tc, tab_words, tab_scales, offs, w1, w2_w
                 nc.scalar.activation(out=th[:, t, :], in_=bank[:], func=TANH)
             return th
 
-        def side_gain(th, place):
-            db = held("db", [P, PACK, HALF], BF16, "ch2_00" if DBHOLD else None)
+        def side_gain(th, place, POOL_GAIN, db_place):
+            db = held("db", [P, PACK, HALF], BF16, db_place)
             for t in range(PACK):
                 if POOL_GAIN == 2:
                     nc.scalar.activation(out=db[:, t, :], in_=th[:, t, :], func=COPY, scale=gain_t[:, t:t + 1])
@@ -258,7 +272,10 @@ def tile_list_relay_forward_log_kernel(tc, tab_words, tab_scales, offs, w1, w2_w
                 for g in range(2):
                     w4_pass(bank[:], g, n, cols, g == 1)
                 nc.scalar.copy(out=y[:, n, :], in_=bank[:])
-            store_y(y, cols)
+                if SPLITY and n % 2:
+                    nc.sync.dma_start(out=out_0[:, cols].rearrange("(n p) j -> p n j", p=P)[:, n - 1:n + 1, :], in_=y[:, n - 1:n + 1, :])
+            if not SPLITY:
+                store_y(y, cols)
 
         def open_narrow(j0):
             bank = next_bank("cy", 8 - AB)
@@ -286,13 +303,12 @@ def tile_list_relay_forward_log_kernel(tc, tab_words, tab_scales, offs, w1, w2_w
         for jh in range(2):
             v[jh] = (v_w[jh], gather("v_s", tab_s[:], U8, jh))
         w1_q[0] = quantize_weight("w1q0", w1_raw[0], "stage_a", "tab_s" if HOLDQ else None)
+        if W2S:
+            deal(nc.vector, w2_s[:], w2_raw_s[:], 1)
         if W3_AT == 0:
             w3_q = quantize_weight("w3q", w3_raw, "stage_b")
         h00 = a_part(0, 0, HALF)
-        if POOL_DEAL:
-            for g in range(2):
-                deal(nc.gpsimd, w2_s[:, span(g)], w2_raw_s[:, span(g)], 1)
-        else:
+        if not W2S:
             deal(nc.vector, w2_s[:], w2_raw_s[:], 1)
         if W3_AT == 3:
             w3_q = quantize_weight("w3q", w3_raw, "stage_b")
@@ -310,7 +326,7 @@ def tile_list_relay_forward_log_kernel(tc, tab_words, tab_scales, offs, w1, w2_w
             th0 = side_tanh(0, w3_q, None)
         h_planes(0, 0, HALF, hb00)
         store_words(0, 0)
-        d0 = side_gain(th0, "stage_b")
+        d0 = side_gain(th0, "stage_b", G0, None)
         th1 = side_tanh(1, w3_q, "th0" if DBHOLD else "ch2_00")
         h10 = a_part(1, 0, HALF)
         hb10 = add_parts(1, 0, HALF, h10, "stage_a")
@@ -318,9 +334,12 @@ def tile_list_relay_forward_log_kernel(tc, tab_words, tab_scales, offs, w1, w2_w
         b_part(0, HALF, HALF)
         h_planes(1, 0, HALF, hb10)
         store_words(1, 0)
-        d1 = side_gain(th1, "stage_a")
+        if YFIRST:
+            forward_wide(span(0))
+        d1 = side_gain(th1, ILD1, G1, DB1)
         h01 = a_part(0, HALF, HALF)
-        forward_wide(span(0))
+        if not YFIRST:
+            forward_wide(span(0))
         hb01 = add_parts(0, HALF, HALF, h01, "stage_b")
         d_planes(1, d1, "ch1_01")
         pieces = [(HALF, 256), (HALF + 256, NARROW), (HALF + 384, NARROW)]
@@ -344,6 +363,5 @@ def tile_list_relay_forward_log_kernel(tc, tab_words, tab_scales, offs, w1, w2_w
         h_planes(1, *pending)
         close_narrow(pending[0], pending[1], True)
         store_words(1, 1)
-        for q in range(4):
-            nc.sync.dma_start(out=out_3[:, 4 * q:4 * q + 4, :].bitcast(I32).rearrange("g q m -> q g m"),
-                              in_=h_s[32 * q:32 * q + 4, :].bitcast(I32).rearrange("p (g m) -> p g m", g=2))
+        for r in range(4):
+            (nc.gpsimd if O3Q else nc.sync).dma_start(out=scale_rows(out_3, r), in_=live_rows(h_s, r, 2))

from contextlib import ExitStack

import concourse.mybir as mybir

K, H, R, N, T, S = 512, 1024, 512, 512, 2048, 1024
FLOPS = 2 * S * (2 * K * H + K * R + H * N + R * N)

F32 = mybir.dt.float32
BF16 = mybir.dt.bfloat16
I32 = mybir.dt.int32
U32 = mybir.dt.uint32
U16 = mybir.dt.uint16
U8 = mybir.dt.uint8
FP8X4 = mybir.dt.float8_e4m3fn_x4
FP4X4 = mybir.dt.float4_e2m1fn_x4
MULT = mybir.AluOpType.mult
ADD = mybir.AluOpType.add
TANH = mybir.ActivationFunctionType.Tanh
COPY = mybir.ActivationFunctionType.Copy

P = 128
PACK = 4
PASS = P * PACK
BANK = 512
HALF = 512
NARROW = 128
POOL_ADD = 0
G0 = 2
G1 = 2
DB1 = None
ILD1 = "stage_a"
O3Q = 0
POOL_DEAL = 0
Y_ON_V = 1
AB = 4
W3_AT = 0
DBHOLD = 0
W2S = 1
SPLITY = 0
POOLQ = 0
YFIRST = 0
ILV = 1
ONEADD = 1
HOLDQ = 1


def tile_list_relay_forward_log_kernel(tc, tab_words, tab_scales, offs, w1, w2_words, w2_scales, w3,
                                                w4_words, w4_scales, w5_words, w5_scales, ch1, ch2, gain,
                                                out_0, out_1, out_2, out_3):
    nc = tc.nc
    with ExitStack() as ctx:
        keep = ctx.enter_context(tc.tile_pool(name="keep", bufs=1))
        psum = ctx.enter_context(tc.psum_pool(name="psum", bufs=1))
        turns = {"ab": [], "cy": []}

        def next_bank(ring, size):
            turns[ring].append(ring)
            return psum.tile([P, BANK], F32, name="%s%d" % (ring, len(turns[ring]) % size))

        def held(name, shape, dtype, place=None):
            return keep.tile(shape, dtype, name=name, tag=place or name, align_bytes=64)

        offsets = keep.tile([P, S // 16], U16, name="offsets")
        tab_w = held("tab_w", [P, T], I32)
        tab_s = held("tab_s", [P, T], U8)
        w2_raw = held("w2_raw", [P, 2 * H], U8)
        w2_raw_s = held("w2_raw_s", [P, H], U8)
        w4_w = held("w4_w", [P, 2 * N], I32)
        w4_s = held("w4_s", [P, 2 * N], U8)
        w5_w = held("w5_w", [P, 2 * N], U8)
        w5_s = held("w5_s", [P, N], U8)
        gain_t = held("gain_t", [P, PACK], F32)

        def live_rows(plane, r, passes):
            return plane[r:P:32, :].bitcast(I32).rearrange("p (a c) -> p a c", a=passes)

        def scale_rows(rows, r):
            return rows[:, r:16:4, :].bitcast(I32).rearrange("a q c -> q a c")

        def load_scales(queue, plane, rows):
            for r in range(4):
                queue.dma_start(out=live_rows(plane, r, rows.shape[0]), in_=scale_rows(rows, r))

        def load_rows(name, src, rows, cols):
            tile = held(name, [P, PACK, HALF], F32)
            nc.sync.dma_start(out=tile[:], in_=src[rows, cols].rearrange("(p t) c -> p t c", t=PACK))
            return tile

        def span(i):
            return slice(i * HALF, (i + 1) * HALF)

        nc.vector.memset(tab_s[:].bitcast(I32), 0)
        nc.vector.memset(w2_raw_s[:].bitcast(I32), 0)
        warm = held("warm", [P, 2], F32)
        nc.gpsimd.memset(warm[:, 0:1], 0.0)
        nc.gpsimd.memset(w5_s[:].bitcast(I32), 0)
        nc.gpsimd.memset(w4_s[:].bitcast(I32), 0)
        nc.scalar.activation(out=warm[:, 1:2], in_=warm[:, 0:1], func=TANH)
        c1, c2, w1_raw = {}, {}, {}
        nc.sync.dma_start(offsets[:], offs)
        nc.sync.dma_start(out=w2_raw[:].bitcast(I32), in_=w2_words[0].bitcast(I32))
        nc.sync.dma_start(out=gain_t[:], in_=gain.rearrange("(p t) -> p t", t=PACK))
        nc.sync.dma_start(out=tab_w[:], in_=tab_words[0].rearrange("p t i -> p (t i)").bitcast(I32))
        nc.sync.dma_start(out=w5_w[:].bitcast(I32), in_=w5_words[0].bitcast(I32))
        w1_raw[0] = load_rows("w1_0", w1, span(0), span(0))
        load_scales(nc.sync, tab_s, tab_scales)
        if W3_AT == 0:
            w3_raw = load_rows("w3_raw", w3, span(0), span(0))
        if W2S:
            load_scales(nc.sync, w2_raw_s, w2_scales)
        c1[0, 0] = load_rows("ch1_00", ch1, span(0), span(0))
        if W3_AT == 3:
            w3_raw = load_rows("w3_raw", w3, span(0), span(0))
        if W3_AT in (1, 2):
            c2[0, 0] = load_rows("ch2_00", ch2, span(0), span(0))
        if not W2S:
            load_scales(nc.sync, w2_raw_s, w2_scales)
        if W3_AT in (0, 3):
            c2[0, 0] = load_rows("ch2_00", ch2, span(0), span(0))
        if W3_AT == 1:
            w3_raw = load_rows("w3_raw", w3, span(0), span(0))
        w1_raw[1] = load_rows("w1_1", w1, span(0), span(1))
        c2[1, 0] = load_rows("ch2_10", ch2, span(1), span(0))
        if W3_AT == 2:
            w3_raw = load_rows("w3_raw", w3, span(0), span(0))
        load_scales(nc.gpsimd if POOLQ else nc.sync, w5_s, w5_scales)
        c1[1, 0] = load_rows("ch1_10", ch1, span(1), span(0))
        c2[0, 1] = load_rows("ch2_01", ch2, span(0), span(1))
        nc.sync.dma_start(out=w4_w[:].rearrange("p (a c) -> p a c", a=2),
                          in_=w4_words.rearrange("a p c i -> p a (c i)").bitcast(I32))
        load_scales(nc.gpsimd if POOLQ else nc.sync, w4_s, w4_scales)
        c1[0, 1] = load_rows("ch1_01", ch1, span(0), span(1))
        c2[1, 1] = load_rows("ch2_11", ch2, span(1), span(1))
        c1[1, 1] = load_rows("ch1_11", ch1, span(1), span(1))

        w2_w = held("w2_w", [P, 2 * H], U8)
        w2_s = held("w2_s", [P, H], U8)

        def deal(engine, dealt, raw, size):
            engine.tensor_copy(out=dealt.rearrange("p (g t m b) -> p g t m b", m=P, t=PACK, b=size),
                               in_=raw.rearrange("p (g m t b) -> p g t m b", m=P, t=PACK, b=size))

        def gather(name, window, dtype, jh):
            picked = held("%s%d" % (name, jh), [P, HALF], dtype)
            nc.vector.tensor_copy(picked[:], window.indirect(offsets[:, jh * HALF // 16:(jh + 1) * HALF // 16]))
            return picked

        def quantize(words, scales, grouped):
            nc.vector.quantize_mx(out=words.bitcast(FP8X4), scales=scales, in_=grouped)

        def staged(place, width):
            tile = held("staged", [P, PACK * width], BF16, place)
            return tile[:]

        def quantize_weight(name, raw, place, words_place=None):
            grouped = staged(place, HALF)
            nc.scalar.copy(out=grouped.rearrange("p (t m i) -> p m i t", t=PACK, i=PACK),
                           in_=raw[:].rearrange("p i (m t) -> p m i t", t=PACK))
            words = held(name + "_w", [P, PASS], U32, words_place)
            scales = held(name + "_s", [P, PASS], U8)
            quantize(words[:], scales[:], grouped)
            return words, scales

        def interleave(rows, width, place, copy=nc.scalar.copy):
            grouped = staged(place, width)
            copy(out=grouped.rearrange("p (c i t) -> p c t i", i=4, t=PACK),
                 in_=rows.rearrange("p t (c i) -> p c t i", i=4))
            return grouped

        def fp8(words, scales, cols):
            return words[:, cols].bitcast(FP8X4), scales[:, cols]

        def fp4(words, scales, cols):
            return words[:, 2 * cols.start:2 * cols.stop].bitcast(FP4X4), scales[:, cols]

        def mm(out, lhs, rhs, start=True, stop=True):
            nc.tensor.matmul_mx(out=out, lhsT=lhs[0], lhsT_scale=lhs[1], rhs=rhs[0], rhs_scale=rhs[1],
                                start=start, stop=stop)

        def times_channel(out, weight, chan, v, cols):
            width = cols.stop - cols.start
            per_bank = BANK // width
            for t0 in range(0, PACK, per_bank):
                bank = next_bank("ab", AB)
                for t in range(per_bank):
                    mm(bank[:, t * width:(t + 1) * width], weight(t0 + t), fp8(v[0], v[1], cols))
                nc.vector.tensor_tensor(out=out[:, t0:t0 + per_bank, :],
                                        in0=bank[:].rearrange("p (t w) -> p t w", t=per_bank),
                                        in1=chan[:, t0:t0 + per_bank, cols], op=MULT)

        h_w = [held("h_w%d" % g, [P, S], U32) for g in range(2)]
        h_s = held("h_s", [P, 2 * S], U8)
        d_w = {}
        d_s = held("d_s", [P, S], U8)
        v, w1_q = {}, {}

        def b_part(g, j0, width):
            jh, cols = j0 // HALF, slice(j0 % HALF, j0 % HALF + width)
            times_channel(c2[g, jh][:, :, cols],
                          lambda t: fp4(w2_w, w2_s, slice(PASS * g + P * t, PASS * g + P * (t + 1))),
                          c2[g, jh], v[jh], cols)

        def a_part(g, j0, width):
            jh, cols = j0 // HALF, slice(j0 % HALF, j0 % HALF + width)
            h = held("h_%d_%d" % (g, j0), [P, PACK, width], F32)
            times_channel(h, lambda t: fp8(w1_q[g][0], w1_q[g][1], slice(P * t, P * (t + 1))),
                          c1[g, jh], v[jh], cols)
            return h

        def add_parts(g, j0, width, h, place):
            jh, cols = j0 // HALF, slice(j0 % HALF, j0 % HALF + width)
            on_pool = POOL_ADD if width == HALF else 0
            for t in range(on_pool):
                nc.gpsimd.tensor_tensor(out=h[:, t, :], in0=h[:, t, :], in1=c2[g, jh][:, t, cols], op=ADD)
            step = PACK if (ONEADD and width < HALF) else 2
            for t0 in range(on_pool, PACK, step):
                t1 = min(t0 + step, PACK)
                nc.vector.tensor_tensor(out=h[:, t0:t1, :], in0=h[:, t0:t1, :],
                                        in1=c2[g, jh][:, t0:t1, cols], op=ADD)
            nc.sync.dma_start(out=out_1[span(g), j0:j0 + width].rearrange("(p t) j -> p t j", t=PACK), in_=h[:])
            if j0 >= S - ILV * NARROW:
                return interleave(h[:], width, place, nc.vector.tensor_copy)
            return interleave(h[:], width, place)

        def h_planes(g, j0, width, grouped):
            quantize(h_w[g][:, j0:j0 + width], h_s[:, S * g + j0:S * g + j0 + width], grouped)

        def store_words(g, jh):
            nc.sync.dma_start(out=out_2[g].rearrange("p m i -> p (m i)").bitcast(I32)[:, span(jh)],
                              in_=h_w[g][:, span(jh)].bitcast(I32))

        def side_tanh(jh, w3_q, place):
            th = held("th%d" % jh, [P, PACK, HALF], F32, place)
            for t in range(PACK):
                bank = next_bank("cy", 8 - AB)
                mm(bank[:], fp8(w3_q[0], w3_q[1], slice(P * t, P * (t + 1))), fp8(v[jh][0], v[jh][1], span(0)))
                nc.scalar.activation(out=th[:, t, :], in_=bank[:], func=TANH)
            return th

        def side_gain(th, place, POOL_GAIN, db_place):
            db = held("db", [P, PACK, HALF], BF16, db_place)
            for t in range(PACK):
                if POOL_GAIN == 2:
                    nc.scalar.activation(out=db[:, t, :], in_=th[:, t, :], func=COPY, scale=gain_t[:, t:t + 1])
                elif POOL_GAIN:
                    nc.gpsimd.tensor_scalar(out=db[:, t, :], in0=th[:, t, :], scalar1=gain_t[:, t:t + 1],
                                            scalar2=0.0, op0=MULT, op1=ADD)
                else:
                    nc.vector.tensor_scalar_mul(out=db[:, t, :], in0=th[:, t, :], scalar1=gain_t[:, t:t + 1])
            return interleave(db[:], HALF, place)

        def d_planes(jh, grouped, place):
            d_w[jh] = held("d_w%d" % jh, [P, HALF], U32, place)
            quantize(d_w[jh][:], d_s[:, span(jh)], grouped)

        def w4_pass(out, g, n, cols, stop):
            mm(out, fp8(w4_w, w4_s, slice(N * g + P * n, N * g + P * (n + 1))),
               (h_w[g][:, cols].bitcast(FP8X4), h_s[:, S * g + cols.start:S * g + cols.stop]), False, stop)

        def w5_pass(out, n, cols, start):
            mm(out, fp4(w5_w, w5_s, slice(P * n, P * (n + 1))),
               (d_w[cols.start // HALF][:, cols.start % HALF:(cols.stop - 1) % HALF + 1].bitcast(FP8X4), d_s[:, cols]), start, False)

        def store_y(y, cols):
            nc.sync.dma_start(out=out_0[:, cols].rearrange("(n p) j -> p n j", p=P), in_=y[:])

        def forward_wide(cols):
            y = held("y_wide", [P, 4, HALF], F32)
            for n in range(4):
                bank = next_bank("cy", 8 - AB)
                w5_pass(bank[:], n, cols, True)
                for g in range(2):
                    w4_pass(bank[:], g, n, cols, g == 1)
                nc.scalar.copy(out=y[:, n, :], in_=bank[:])
                if SPLITY and n % 2:
                    nc.sync.dma_start(out=out_0[:, cols].rearrange("(n p) j -> p n j", p=P)[:, n - 1:n + 1, :], in_=y[:, n - 1:n + 1, :])
            if not SPLITY:
                store_y(y, cols)

        def open_narrow(j0):
            bank = next_bank("cy", 8 - AB)
            cols = slice(j0, j0 + NARROW)
            for n in range(4):
                w5_pass(bank[:, n * NARROW:(n + 1) * NARROW], n, cols, n == 0)
            for n in range(4):
                w4_pass(bank[:, n * NARROW:(n + 1) * NARROW], 0, n, cols, False)
            return bank

        def close_narrow(j0, width, last):
            y = held("y_%d" % j0, [P, 4, width], F32)
            for c0 in range(0, width, NARROW):
                bank = narrow[j0 + c0]
                for n in range(4):
                    w4_pass(bank[:, n * NARROW:(n + 1) * NARROW], 1, n, slice(j0 + c0, j0 + c0 + NARROW), n == 3)
                if last and Y_ON_V:
                    nc.vector.tensor_copy(out=y[:, :, c0:c0 + NARROW], in_=bank[:].rearrange("p (n w) -> p n w", n=4))
                else:
                    nc.scalar.copy(out=y[:, :, c0:c0 + NARROW], in_=bank[:].rearrange("p (n w) -> p n w", n=4))
            store_y(y, slice(j0, j0 + width))

        deal(nc.vector, w2_w[:], w2_raw[:], 2)
        v_w = [gather("v_w", tab_w[:].bitcast(U32), U32, jh) for jh in range(2)]
        for jh in range(2):
            v[jh] = (v_w[jh], gather("v_s", tab_s[:], U8, jh))
        w1_q[0] = quantize_weight("w1q0", w1_raw[0], "stage_a", "tab_s" if HOLDQ else None)
        if W2S:
            deal(nc.vector, w2_s[:], w2_raw_s[:], 1)
        if W3_AT == 0:
            w3_q = quantize_weight("w3q", w3_raw, "stage_b")
        h00 = a_part(0, 0, HALF)
        if not W2S:
            deal(nc.vector, w2_s[:], w2_raw_s[:], 1)
        if W3_AT == 3:
            w3_q = quantize_weight("w3q", w3_raw, "stage_b")
        if W3_AT in (0, 3):
            th0 = side_tanh(0, w3_q, None)
        b_part(0, 0, HALF)
        if W3_AT == 1:
            w3_q = quantize_weight("w3q", w3_raw, "stage_c", "ch1_00")
        w1_q[1] = quantize_weight("w1q1", w1_raw[1], "stage_a")
        hb00 = add_parts(0, 0, HALF, h00, "stage_b")
        if W3_AT == 2:
            w3_q = quantize_weight("w3q", w3_raw, "stage_c", "ch1_00")
        b_part(1, 0, HALF)
        if W3_AT in (1, 2):
            th0 = side_tanh(0, w3_q, None)
        h_planes(0, 0, HALF, hb00)
        store_words(0, 0)
        d0 = side_gain(th0, "stage_b", G0, None)
        th1 = side_tanh(1, w3_q, "th0" if DBHOLD else "ch2_00")
        h10 = a_part(1, 0, HALF)
        hb10 = add_parts(1, 0, HALF, h10, "stage_a")
        d_planes(0, d0, "ch1_10")
        b_part(0, HALF, HALF)
        h_planes(1, 0, HALF, hb10)
        store_words(1, 0)
        if YFIRST:
            forward_wide(span(0))
        d1 = side_gain(th1, ILD1, G1, DB1)
        h01 = a_part(0, HALF, HALF)
        if not YFIRST:
            forward_wide(span(0))
        hb01 = add_parts(0, HALF, HALF, h01, "stage_b")
        d_planes(1, d1, "ch1_01")
        pieces = [(HALF, 256), (HALF + 256, NARROW), (HALF + 384, NARROW)]
        pending = None
        narrow = {}
        for j0, width in pieces:
            b_part(1, j0, width)
            if pending is None:
                h_planes(0, HALF, HALF, hb01)
                store_words(0, 1)
            h = a_part(1, j0, width)
            if pending is not None:
                h_planes(1, *pending)
            grouped = add_parts(1, j0, width, h, "stage_%d" % j0)
            if pending is None:
                for c0 in range(HALF, S, NARROW):
                    narrow[c0] = open_narrow(c0)
            else:
                close_narrow(pending[0], pending[1], False)
            pending = (j0, width, grouped)
        h_planes(1, *pending)
        close_narrow(pending[0], pending[1], True)
        store_words(1, 1)
        for r in range(4):
            (nc.gpsimd if O3Q else nc.sync).dma_start(out=scale_rows(out_3, r), in_=live_rows(h_s, r, 2))
